import numpy as np
import ml_dtypes


def mxq(x, axis, fmt="e4m3"):
    dtype, down = {"e4m3": (ml_dtypes.float8_e4m3fn, 7), "e5m2": (ml_dtypes.float8_e5m2, 14)}[fmt]
    v = np.moveaxis(np.asarray(x, np.float32).astype(ml_dtypes.bfloat16).astype(np.float64), axis, -1)
    blocks = v.reshape(v.shape[:-1] + (-1, 32))
    amax = np.abs(blocks).max(-1, keepdims=True)
    byte = np.maximum(np.where(amax > 0, np.frexp(amax)[1] - 1 + 127, 0) - down, 1)
    scale = np.exp2(byte - 127.0)
    codes = (blocks / scale).astype(np.float32).astype(dtype).astype(np.float64)
    return np.moveaxis((codes * scale).reshape(v.shape), -1, axis)


WIDE = False


def mx_kscale(k):
    if not WIDE:
        return np.ones(k)
    levels = np.array([10, -10, 5, -5, 0])
    if k % 512:
        return np.exp2(np.random.permutation(np.resize(levels, k // 32))).repeat(32)
    a = np.empty((k // 512, 16))
    for p in range(k // 512):
        a[p, :8] = np.random.permutation(np.resize(levels, 8))
        for g in range(8):
            far = levels[np.abs(levels - a[p, g]) >= 10]
            a[p, g + 8] = far[np.random.randint(len(far))]
    return np.exp2(a.ravel()).repeat(32)


def f64(x):
    return np.asarray(x).astype(np.float64)


def striped(idx):
    return np.tile(idx.reshape(-1, 16).T, (8, 1)).astype(np.uint16)


def unstriped(offs):
    return offs[:16].T.reshape(-1).astype(np.int64)


def pack_weight(w):
    k, n = w.shape
    w = f64(np.asarray(w, np.float32).astype(ml_dtypes.bfloat16)).reshape(k // 32, 32, n)
    amax = np.abs(w).max(1)
    byte = np.clip(np.where(amax > 0, np.frexp(amax)[1] - 1 + 127 - 7, 1), 1, 254)
    scaled = (w * np.exp2(127.0 - byte)[:, None, :]).reshape(k, n).astype(np.float32)
    words = np.ascontiguousarray(scaled.reshape(k // 512, 128, 4, n).transpose(0, 1, 3, 2)).astype(ml_dtypes.float8_e4m3fn).view(np.uint8)
    return words, np.ascontiguousarray(byte.astype(np.uint8).reshape(k // 512, 16, n))


def unpack_weight(words, scales):
    g, p, n, _ = words.shape
    vals = np.ascontiguousarray(words).view(ml_dtypes.float8_e4m3fn).astype(np.float64) * np.repeat(np.exp2(scales.astype(np.float64) - 127.0), 8, axis=1)[..., None]
    return vals.transpose(0, 1, 3, 2).reshape(g * 512, n)


K, T, S, N, H, W = 512, 2048, 512, 512, 512, 384


def setup_inputs():
    n = np.random.standard_normal
    s = mx_kscale(K)[:, None]
    u = mx_kscale(H)
    packed_xT = pack_weight(n((K, T)) * s)
    return {
        "x_words": packed_xT[0],
        "x_scales": packed_xT[1],
        "w1": (n((K, H)) / np.sqrt(K) / s).astype(np.float32),
        "tau": np.random.uniform(0.3, 0.9, (H, 1)).astype(np.float32),
        "tau2": np.random.uniform(0.3, 0.9, (H, 1)).astype(np.float32),
        "gn": (np.random.uniform(0.5, 1.5, (H, 1)) * u[:, None]).astype(np.float32),
        "gm": (np.random.uniform(0.5, 1.5, (H, 1)) * u[:, None]).astype(np.float32),
        "w2": (n((H, N)) / np.sqrt(2 * H) / u[:, None]).astype(np.float32),
        "w3": (n((H, N)) / np.sqrt(2 * H) / u[:, None]).astype(np.float32),
        "tau3": np.random.uniform(0.5, 1.2, (N, 1)).astype(np.float32),
        "offs": striped(np.random.permutation(T)[:S]),
        "n1": striped(np.random.permutation(S)[:W]),
        "n2": striped(np.random.permutation(S)[:W]),
        "n3": striped(np.random.permutation(S)),
        "n4": striped(np.random.permutation(S)),
        "n5": striped(np.random.permutation(S)),
        "n6": striped(np.random.permutation(S)),
    }


def reference(x_words, x_scales, w1, tau, tau2, gn, gm, w2, w3, tau3, offs, n1, n2, n3, n4, n5, n6):
    xq = unpack_weight(x_words, x_scales)[:, unstriped(offs)]
    y = mxq(f64(w1), 0, "e4m3").T @ xq
    pa = y[:, unstriped(n2)]
    old = y[:, unstriped(n1)]
    ra = np.maximum(pa, 0.5 * old)
    ds = y.copy()
    ds[:, unstriped(n1)] = ra
    z = f64(gn) * ds
    top = y.max(axis=1, keepdims=True)
    ea = np.exp(f64(tau) * (y[:, unstriped(n3)] - top))
    low = y.min(axis=1, keepdims=True)
    ea2 = np.exp(f64(tau2) * (low - y[:, unstriped(n4)]))
    z2 = f64(gm) * (1.5 * (y * (ea + ea2)))
    h = mxq(f64(w2), 0, "e4m3").T @ mxq(z, 0, "e4m3") + mxq(f64(w3), 0, "e4m3").T @ mxq(z2, 0, "e4m3")
    sz = np.abs(h)
    ea3 = np.exp(-1.0 * (f64(tau3) * sz[:, unstriped(n5)]))
    return (h - h[:, unstriped(n6)]) * ea3

from contextlib import ExitStack

import concourse.mybir as mybir

K, T, S, N, H, W = 512, 2048, 512, 512, 512, 384
FLOPS = 3 * 2 * 512 * 512 * 512

F32 = mybir.dt.float32
BF16 = mybir.dt.bfloat16
I32 = mybir.dt.int32
U32 = mybir.dt.uint32
U16 = mybir.dt.uint16
U8 = mybir.dt.uint8
FP8X4 = mybir.dt.float8_e4m3fn_x4
ALU = mybir.AluOpType
ACT = mybir.ActivationFunctionType

P = 128
PACK = 4
HALF = S // 2
LIST_HALF = HALF // 16


def tile_picked_joinkmaxedfela_none_p_kernel(
    tc, x_words, x_scales, w1, tau, tau2, gn, gm, w2, w3, tau3, offs, n1, n2, n3, n4, n5, n6, out
):
    nc = tc.nc
    with ExitStack() as ctx:
        keep = ctx.enter_context(tc.tile_pool(name="keep", bufs=1))
        psum = ctx.enter_context(tc.psum_pool(name="psum", bufs=1))

        def sb(name, shape, dtype, tag=None):
            return keep.tile(shape, dtype, name=name, tag=tag or name, align_bytes=64)

        def load_list(name, src):
            tile = keep.tile(list(src.shape), U16, name=name)
            nc.sync.dma_start(tile[:], src)
            return tile

        def halves():
            return [(slice(a * HALF, (a + 1) * HALF), slice(a * LIST_HALF, (a + 1) * LIST_HALF)) for a in range(2)]

        xw = sb("xw", [P, T], I32)
        xs = sb("xs", [P, T], U8)
        nc.gpsimd.memset(xs[:].bitcast(I32), 0)
        nc.sync.dma_start(xw[:], x_words[0].rearrange("p c r -> p (c r)").bitcast(I32))
        offs_t = load_list("offs_t", offs)
        for q in range(4):
            nc.scalar.dma_start(xs[32 * q : 32 * q + 4, :].bitcast(I32), x_scales[0, 4 * q : 4 * q + 4, :].bitcast(I32))
        w1_rows = w1.rearrange("(p j) c -> p j c", j=PACK)
        w1_raw = [sb(f"w1_raw{a}", [P, PACK, HALF], F32) for a in range(2)]
        for a in range(2):
            nc.sync.dma_start(w1_raw[a][:], w1_rows[:, :, a * HALF : (a + 1) * HALF])
        n2_t = load_list("n2_t", n2)
        n1_t = load_list("n1_t", n1)
        n3_t = load_list("n3_t", n3)
        n4_t = load_list("n4_t", n4)

        def load_col(name, src):
            tile = sb(name, [P, PACK], F32)
            nc.gpsimd.dma_start(tile[:], src.rearrange("(p t) o -> p (t o)", t=PACK))
            return tile

        tau_t = load_col("tau_t", tau)
        tau2_t = load_col("tau2_t", tau2)
        gm_t = load_col("gm_t", gm)
        gn_t = load_col("gn_t", gn)
        w2_raw = sb("w2_raw", [P, PACK, N], F32)
        w3_raw = sb("w3_raw", [P, PACK, N], F32)
        nc.sync.dma_start(w2_raw[:], w2.rearrange("(p j) c -> p j c", j=PACK))
        nc.sync.dma_start(w3_raw[:], w3.rearrange("(p j) c -> p j c", j=PACK))
        n5_t = load_list("n5_t", n5)
        n6_t = load_list("n6_t", n6)
        tau3_t = sb("tau3_t", [P, PACK], F32)
        with nc.allow_non_contiguous_dma(reason="one rate a partition and tile"):
            nc.sync.dma_start(tau3_t[:], tau3.rearrange("(t p) o -> p (t o)", p=P))

        rate = sb("rate", [P, PACK, 2], F32)
        ntau2 = sb("ntau2", [P, PACK], F32)
        gm15 = sb("gm15", [P, PACK], F32)
        ntau3 = sb("ntau3", [P, PACK], F32)
        nc.gpsimd.tensor_scalar(rate[:, :, 0], tau_t[:], -1.0, 0.0, ALU.mult, ALU.add)
        nc.gpsimd.tensor_scalar(rate[:, :, 1], tau2_t[:], 1.0, 0.0, ALU.mult, ALU.add)
        nc.gpsimd.tensor_scalar(ntau2[:], tau2_t[:], -1.0, 0.0, ALU.mult, ALU.add)
        nc.gpsimd.tensor_scalar(gm15[:], gm_t[:], 1.5, 0.0, ALU.mult, ALU.add)
        nc.gpsimd.tensor_scalar(ntau3[:], tau3_t[:], -1.0, 0.0, ALU.mult, ALU.add)

        xg_w = sb("xg_w", [P, S], U32)
        xg_s = sb("xg_s", [P, S], U8)
        nc.vector.tensor_copy(xg_w[:], xw[:].bitcast(U32).indirect(offs_t[:]))
        nc.vector.tensor_copy(xg_s[:], xs[:].indirect(offs_t[:]))

        w1_bf = sb("w1_bf", [P, PACK * H], BF16)
        w1_dst = w1_bf[:].rearrange("p (t m j) -> p m j t", t=PACK, j=PACK)
        nc.scalar.copy(w1_dst[:, 0:64], w1_raw[0][:].rearrange("p j (m t) -> p m j t", t=PACK))
        w1_hi = w1_raw[1][:].rearrange("p j (m t) -> p m j t", t=PACK)
        nc.scalar.copy(w1_dst[:, 64:88], w1_hi[:, 0:24])
        nc.vector.tensor_copy(w1_dst[:, 88:128], w1_hi[:, 24:64])
        w1_c = sb("w1_c", [P, H], U32)
        w1_s = sb("w1_s", [P, H], U8)
        nc.vector.quantize_mx(out=w1_c[:, 0:P].bitcast(FP8X4), scales=w1_s[:, 0:P], in_=w1_bf[:, 0 : PACK * P])
        nc.vector.quantize_mx(out=w1_c[:, P:H].bitcast(FP8X4), scales=w1_s[:, P:H], in_=w1_bf[:, PACK * P :])

        y_ps = [psum.tile([P, S], F32, name=f"y_ps{t}") for t in range(PACK)]
        for t in range(PACK):
            cols = slice(t * P, (t + 1) * P)
            nc.tensor.matmul_mx(
                out=y_ps[t][:], lhsT=w1_c[:, cols].bitcast(FP8X4), lhsT_scale=w1_s[:, cols],
                rhs=xg_w[:].bitcast(FP8X4), rhs_scale=xg_s[:], start=True, stop=True,
            )

        y_sb = [sb(f"y_sb{t}", [P, S], F32) for t in range(PACK)]
        ds = [sb(f"ds{t}", [P, S], F32) for t in range(PACK)]
        ext = [sb(f"ext{t}", [P, 2], F32) for t in range(PACK)]
        bias = [sb(f"bias{t}", [P, 2], F32) for t in range(PACK)]
        pa = [sb(f"pa{t}", [P, W], F32) for t in range(PACK)]
        old = [sb(f"old{t}", [P, W], F32) for t in range(PACK)]
        ra = [sb(f"ra{t}", [P, W], F32) for t in range(PACK)]
        ea = [sb("ea0", [P, S], F32)[:]]
        ea2 = [sb("ea2_0", [P, S], F32)[:]]
        es = [sb(f"es{t}", [P, S], F32) for t in range(PACK)]
        z_pl = sb("z_pl", [P, PACK, S], BF16)
        z2_pl = sb("z2_pl", [P, PACK, S], BF16)
        z_il = sb("z_il", [P, PACK * S], BF16)
        z2_il = sb("z2_il", [P, PACK * S], BF16)
        z_c, z_s = sb("z_c", [P, S], U32), sb("z_s", [P, S], U8)
        z2_c, z2_s = sb("z2_c", [P, S], U32), sb("z2_s", [P, S], U8)
        w2_bf, w3_bf = sb("w2_bf", [P, PACK * N], BF16), sb("w3_bf", [P, PACK * N], BF16)
        w2_c, w2_s = sb("w2_c", [P, N], U32), sb("w2_s", [P, N], U8)
        w3_c, w3_s = sb("w3_c", [P, N], U32), sb("w3_s", [P, N], U8)

        def evac_top(t):
            nc.vector.tensor_scalar(y_sb[t][:], y_ps[t][:], 1.0, None, ALU.mult, ALU.max, accum_out=ext[t][:, 0:1])

        def evac_low(t):
            nc.vector.tensor_scalar(ds[t][:], y_ps[t][:], 1.0, None, ALU.mult, ALU.min, accum_out=ext[t][:, 1:2])

        def biases(t):
            nc.vector.tensor_tensor(bias[t][:], ext[t][:], rate[:, t, :], ALU.mult)

        def fetch(dst, window, offsets, on_scalar):
            if on_scalar:
                nc.scalar.activation(dst, window.indirect(offsets), ACT.Copy)
            else:
                nc.vector.tensor_copy(dst, window.indirect(offsets))

        def larger(t):
            nc.vector.scalar_tensor_tensor(ra[t][:], old[t][:], 0.5, pa[t][:], ALU.mult, ALU.max)

        def put_back(t):
            nc.scalar.activation(ds[t][:].indirect(n1_t[:]), ra[t][:], ACT.Copy)

        def exp_top(t, cols, lst):
            nc.scalar.activation(ea[t][:, cols], y_sb[t][:].indirect(n3_t[:, lst]), ACT.Exp,
                                 bias=bias[t][:, 0:1], scale=tau_t[:, t : t + 1])

        def exp_low(t, cols, lst):
            nc.scalar.activation(ea2[t][:, cols], y_sb[t][:].indirect(n4_t[:, lst]), ACT.Exp,
                                 bias=bias[t][:, 1:2], scale=ntau2[:, t : t + 1])

        def exps(t):
            for cols, lst in halves():
                exp_top(t, cols, lst)
                exp_low(t, cols, lst)

        def add_exps(t, cols):
            nc.vector.tensor_tensor(es[t][:, cols], ea[t][:, cols], ea2[t][:, cols], ALU.add)

        def make_z2(t, cols):
            nc.vector.scalar_tensor_tensor(z2_pl[:, t, cols], es[t][:, cols], gm15[:, t : t + 1], y_ps[t][:, cols],
                                           ALU.mult, ALU.mult)

        def make_z(t):
            nc.vector.tensor_scalar(z_pl[:, t, :], ds[t][:], gn_t[:, t : t + 1], None, ALU.mult)

        def interleave(dst, src, cols):
            nc.vector.tensor_copy(
                dst[:, PACK * cols.start : PACK * cols.stop].rearrange("p (c i t) -> p c t i", i=4, t=PACK),
                src[:, :, cols].rearrange("p t (c i) -> p c t i", i=4),
            )

        def quantize(codes, scales, src, cols):
            nc.vector.quantize_mx(out=codes[:, cols].bitcast(FP8X4), scales=scales[:, cols],
                                  in_=src[:, PACK * cols.start : PACK * cols.stop])

        whole = slice(0, S)
        evac_top(0)
        fetch(pa[0][:], y_sb[0][:], n2_t[:], True)
        fetch(old[0][:], y_sb[0][:], n1_t[:], True)
        evac_low(0)
        evac_top(1)
        biases(0)
        fetch(pa[1][:], y_sb[1][:], n2_t[:], False)
        larger(0)
        for cols, lst in halves():
            exp_top(0, cols, lst)
        put_back(0)
        fetch(old[1][:], y_sb[1][:], n1_t[:], False)
        evac_low(1)
        larger(1)
        put_back(1)
        evac_top(2)
        fetch(pa[2][:], y_sb[2][:], n2_t[:], False)
        fetch(old[2][:], y_sb[2][:], n1_t[:], False)
        evac_top(3)
        larger(2)
        evac_low(2)
        fetch(pa[3][:], y_sb[3][:], n2_t[:], True)
        put_back(2)
        fetch(old[3][:], y_sb[3][:], n1_t[:], False)
        evac_low(3)
        larger(3)
        for cols, lst in halves():
            exp_low(0, cols, lst)
        put_back(3)
        for t in range(1, PACK):
            biases(t)
        late = sb("late", [P, 2 * (PACK - 1), S], F32, tag="ra3")
        for t in range(1, PACK):
            ea.append(late[:, 2 * t - 2, :])
            ea2.append(late[:, 2 * t - 1, :])
        interleave(w2_bf, w2_raw, whole)
        make_z(0)
        quantize(w2_c, w2_s, w2_bf, whole)
        make_z(1)
        add_exps(0, whole)
        make_z(2)
        make_z2(0, whole)
        make_z(3)
        interleave(w3_bf, w3_raw, whole)
        interleave(z_il, z_pl, whole)
        quantize(w3_c, w3_s, w3_bf, whole)
        quantize(z_c, z_s, z_il, whole)

        h_ps = [psum.tile([P, S], F32, name=f"h_ps{m}") for m in range(PACK)]

        def product(m, wc, ws, zc, zs, cols, start, stop):
            mc = slice(m * P, (m + 1) * P)
            nc.tensor.matmul_mx(
                out=h_ps[m][:, cols], lhsT=wc[:, mc].bitcast(FP8X4), lhsT_scale=ws[:, mc],
                rhs=zc[:, cols].bitcast(FP8X4), rhs_scale=zs[:, cols], start=start, stop=stop,
            )

        for m in range(PACK):
            product(m, w2_c, w2_s, z_c, z_s, whole, True, False)

        for a, (cols, lst) in enumerate(halves()):
            for t in range(1, PACK):
                exp_top(t, cols, lst)
                exp_low(t, cols, lst)
                add_exps(t, cols)
                make_z2(t, cols)
            interleave(z2_il, z2_pl, cols)
            quantize(z2_c, z2_s, z2_il, cols)
            for m in range(PACK):
                product(m, w3_c, w3_s, z2_c, z2_s, cols, False, a == 1)

        h_sb = [sb(f"h_sb{m}", [P, S], F32) for m in range(PACK)]
        h_two = [sb(f"h_two{m}", [P, S], F32) for m in range(PACK)]
        sz = [sb(f"sz{m}", [P, S], F32) for m in range(PACK)]
        ea3 = [sb(f"ea3_{m}", [P, S], F32) for m in range(PACK)]
        diff = [sb(f"diff{m}", [P, S], F32) for m in range(PACK)]
        res = [sb(f"res{m}", [P, S], F32) for m in range(PACK)]

        def size(m):
            nc.scalar.activation(sz[m][:], h_ps[m][:], ACT.Abs)

        def decay(m):
            for cols, lst in halves():
                nc.scalar.activation(ea3[m][:, cols], sz[m][:].indirect(n5_t[:, lst]), ACT.Exp,
                                     scale=ntau3[:, m : m + 1])

        def difference(m):
            nc.vector.tensor_copy(h_two[m][:], h_sb[m][:])
            for cols, lst in halves():
                nc.vector.tensor_tensor(diff[m][:, cols], h_sb[m][:].indirect(n6_t[:, lst]), h_two[m][:, cols],
                                        ALU.subtract)

        def finish(m):
            for cols, lst in halves():
                nc.vector.scalar_tensor_tensor(res[m][:, cols], diff[m][:, cols], -1.0, ea3[m][:, cols],
                                               ALU.mult, ALU.mult)
                nc.sync.dma_start(out[m * P : (m + 1) * P, cols], res[m][:, cols])

        size(0)
        nc.vector.tensor_copy(h_sb[1][:], h_ps[1][:])
        nc.vector.tensor_copy(h_sb[0][:], h_ps[0][:])
        decay(0)
        difference(0)
        size(1)
        decay(1)
        finish(0)
        nc.scalar.copy(h_sb[2][:], h_ps[2][:])
        difference(1)
        size(2)
        finish(1)
        nc.scalar.copy(h_sb[3][:], h_ps[3][:])
        decay(2)
        difference(2)
        size(3)
        finish(2)
        decay(3)
        difference(3)
        finish(3)
